import numpy as np
import ml_dtypes


def mxq(x, axis, fmt="e4m3"):
    dtype, down = {"e4m3": (ml_dtypes.float8_e4m3fn, 7), "e5m2": (ml_dtypes.float8_e5m2, 14)}[fmt]
    v = np.moveaxis(np.asarray(x, np.float32).astype(ml_dtypes.bfloat16).astype(np.float64), axis, -1)
    blocks = v.reshape(v.shape[:-1] + (-1, 32))
    amax = np.abs(blocks).max(-1, keepdims=True)
    byte = np.maximum(np.where(amax > 0, np.frexp(amax)[1] - 1 + 127, 0) - down, 1)
    scale = np.exp2(byte - 127.0)
    codes = (blocks / scale).astype(np.float32).astype(dtype).astype(np.float64)
    return np.moveaxis((codes * scale).reshape(v.shape), -1, axis)


WIDE = False


def mx_kscale(k):
    if not WIDE:
        return np.ones(k)
    levels = np.array([10, -10, 5, -5, 0])
    if k % 512:
        return np.exp2(np.random.permutation(np.resize(levels, k // 32))).repeat(32)
    a = np.empty((k // 512, 16))
    for p in range(k // 512):
        a[p, :8] = np.random.permutation(np.resize(levels, 8))
        for g in range(8):
            far = levels[np.abs(levels - a[p, g]) >= 10]
            a[p, g + 8] = far[np.random.randint(len(far))]
    return np.exp2(a.ravel()).repeat(32)


def f64(x):
    return np.asarray(x).astype(np.float64)


def striped(idx):
    return np.tile(idx.reshape(-1, 16).T, (8, 1)).astype(np.uint16)


def unstriped(offs):
    return offs[:16].T.reshape(-1).astype(np.int64)


def striped8(idx):
    return np.concatenate([x.reshape(-1, 16).T for x in idx]).astype(np.uint16)


def runs(offs, k):
    lists = np.stack([offs[16 * r : 16 * r + 16].T.reshape(-1) for r in range(8)]).astype(np.int64)
    return lists[np.arange(k) % 512 // 64]


def pack_weight(w):
    k, n = w.shape
    w = f64(np.asarray(w, np.float32).astype(ml_dtypes.bfloat16)).reshape(k // 32, 32, n)
    amax = np.abs(w).max(1)
    byte = np.clip(np.where(amax > 0, np.frexp(amax)[1] - 1 + 127 - 7, 1), 1, 254)
    scaled = (w * np.exp2(127.0 - byte)[:, None, :]).reshape(k, n).astype(np.float32)
    words = np.ascontiguousarray(scaled.reshape(k // 512, 128, 4, n).transpose(0, 1, 3, 2)).astype(ml_dtypes.float8_e4m3fn).view(np.uint8)
    return words, np.ascontiguousarray(byte.astype(np.uint8).reshape(k // 512, 16, n))


def unpack_weight(words, scales):
    g, p, n, _ = words.shape
    vals = np.ascontiguousarray(words).view(ml_dtypes.float8_e4m3fn).astype(np.float64) * np.repeat(np.exp2(scales.astype(np.float64) - 127.0), 8, axis=1)[..., None]
    return vals.transpose(0, 1, 3, 2).reshape(g * 512, n)


K, T, S, N, H = 512, 2048, 256, 512, 512


def setup_inputs():
    n = np.random.standard_normal
    s = mx_kscale(K)[:, None]
    u = mx_kscale(H)
    packed_xT = pack_weight(n((K, T)) * s)
    return {
        "x_words": packed_xT[0],
        "x_scales": packed_xT[1],
        "w1": (n((K, H)) / np.sqrt(K) / s).astype(np.float32),
        "gn": (np.random.uniform(0.5, 1.5, (H, 1)) * u[:, None]).astype(np.float32),
        "w2": (n((H, N)) / np.sqrt(H) / u[:, None]).astype(np.float32),
        "w3": (n((K, N)) / np.sqrt(K) / s).astype(np.float32),
        "offs": striped(np.random.permutation(T)[:S]),
        "n1": striped8(np.stack([np.random.permutation(S) for _ in range(8)])),
        "n2": striped8(np.stack([np.random.permutation(S) for _ in range(8)])),
        "two": striped(np.random.permutation(T)[:S]),
        "n3": striped(np.random.permutation(S)),
        "n4": striped(np.random.permutation(S)),
        "n5": striped(np.random.permutation(S)),
    }


def reference(x_words, x_scales, w1, gn, w2, w3, offs, n1, n2, two, n3, n4, n5):
    xq = unpack_weight(x_words, x_scales)[:, unstriped(offs)]
    y = mxq(f64(w1), 0, "e4m3").T @ xq
    st = y + 0.5 * (y[np.arange(H)[:, None], runs(n1, H)])
    z = f64(gn) * (st - (st[np.arange(H)[:, None], runs(n2, H)]))
    h = mxq(f64(w2), 0, "e4m3").T @ mxq(z, 0, "e4m3")
    x_two = unpack_weight(x_words, x_scales)[:, unstriped(two)]
    d = mxq(f64(w3), 0, "e4m3").T @ x_two
    return np.maximum(np.minimum(h - (0.5 * h[:, unstriped(n3)]), d[:, unstriped(n4)]), d[:, unstriped(n5)])

@@ -1,0 +1,152 @@
+from contextlib import ExitStack
+
+import concourse.mybir as mybir
+
+F32 = mybir.dt.float32
+BF16 = mybir.dt.bfloat16
+I32 = mybir.dt.int32
+U32 = mybir.dt.uint32
+U16 = mybir.dt.uint16
+U8 = mybir.dt.uint8
+FP8X4 = mybir.dt.float8_e4m3fn_x4
+ALU = mybir.AluOpType
+COPY = mybir.ActivationFunctionType.Copy
+
+P = 128
+K, T, S, N, H = 512, 2048, 256, 512, 512
+FLOPS = 2 * S * (K * H + H * N + K * N)
+W8 = 512
+W1 = 352
+
+
+def tile_picked_lateclampbhop_none_p_kernel(tc, x_words, x_scales, w1, gn, w2, w3, offs, n1, n2, two, n3, n4, n5, out):
+    nc = tc.nc
+    with ExitStack() as ctx:
+        sb = ctx.enter_context(tc.tile_pool(name="sb", bufs=1))
+        ps = ctx.enter_context(tc.psum_pool(name="ps", bufs=1))
+
+        def load_list(ap, name):
+            t = sb.tile([P, S // 16], U16, name=name)
+            nc.sync.dma_start(t[:], ap)
+            return t
+
+        def load_weight(w, name):
+            t = sb.tile([P, 4, 512], F32, name=name)
+            nc.sync.dma_start(t[:], w.rearrange("(p j) c -> p j c", j=4))
+            return t
+
+        xs = sb.tile([P, T], U8, name="xs", align_bytes=64)
+        nc.vector.memset(xs[:].bitcast(I32), 0)
+        for q in range(4):
+            nc.scalar.dma_start(xs[32 * q : 32 * q + 4, :].bitcast(I32), x_scales[0, 4 * q : 4 * q + 4, :].bitcast(I32))
+
+        l_offs = load_list(offs, "l_offs")
+        l_two = load_list(two, "l_two")
+        w1_raw = load_weight(w1, "w1_raw")
+        xw = sb.tile([P, T], I32, name="xw", align_bytes=64)
+        nc.sync.dma_start(xw[:], x_words[0].rearrange("p n t -> p (n t)").bitcast(I32))
+        gain = sb.tile([P, 4], F32, name="gain")
+        nc.sync.dma_start(gain[:], gn.rearrange("(p t) o -> p (t o)", t=4))
+        l_n1 = load_list(n1, "l_n1")
+        w3_raw = load_weight(w3, "w3_raw")
+        l_n2 = load_list(n2, "l_n2")
+        w2_raw = load_weight(w2, "w2_raw")
+        l_n5 = load_list(n5, "l_n5")
+        l_n4 = load_list(n4, "l_n4")
+        l_n3 = load_list(n3, "l_n3")
+
+        y_win = [sb.tile([P, W8], F32, name=f"y_win{t}") for t in range(4)]
+        st_win = [sb.tile([P, W8], F32, name=f"st_win{t}") for t in range(4)]
+        d_win = [sb.tile([P, W1], F32, name=f"d_win{t}") for t in range(4)]
+        h_win = [sb.tile([P, W1], F32, name=f"h_win{t}") for t in range(4)]
+        for win in y_win + d_win + h_win:
+            nc.vector.memset(win[:, S:], 0.0)
+
+        def pick_scales(lst, name):
+            t = sb.tile([P, S], U8, name=name, align_bytes=64)
+            nc.vector.tensor_copy(t[:], xs[:].indirect(lst[:]))
+            return t
+
+        def pick_words(lst, name):
+            t = sb.tile([P, S], U32, name=name, align_bytes=64)
+            nc.vector.tensor_copy(t[:], xw[:].bitcast(U32).indirect(lst[:]))
+            return t
+
+        def quantize(src, name):
+            n = src.shape[1] // 4
+            codes = sb.tile([P, n], U32, name=name + "_codes", align_bytes=64)
+            scales = sb.tile([P, n], U8, name=name + "_scales", align_bytes=64)
+            nc.vector.quantize_mx(out=codes[:].bitcast(FP8X4), scales=scales[:], in_=src[:])
+            return codes, scales
+
+        def product(acc, lhs, cols, rhs):
+            nc.tensor.matmul_mx(out=acc, lhsT=lhs[0][:, cols].bitcast(FP8X4), lhsT_scale=lhs[1][:, cols],
+                                rhs=rhs[0][:].bitcast(FP8X4), rhs_scale=rhs[1][:], start=True, stop=True)
+
+        def round_block(raw, u, name):
+            t = sb.tile([P, 512], BF16, name=name, align_bytes=64)
+            nc.vector.tensor_copy(t[:].rearrange("p (c i j) -> p c j i", i=4, j=4),
+                                  raw[:, :, P * u : P * (u + 1)].rearrange("p j (c i) -> p c j i", i=4))
+            return t
+
+        xo_scales = pick_scales(l_offs, "xo_scales")
+        xt_scales = pick_scales(l_two, "xt_scales")
+
+        w1_bf = sb.tile([P, 2048], BF16, name="w1_bf", align_bytes=64)
+        nc.vector.tensor_copy(w1_bf[:].rearrange("p (t m j) -> p m j t", t=4, j=4),
+                              w1_raw[:].rearrange("p j (m t) -> p m j t", t=4))
+        w1_q = quantize(w1_bf, "w1")
+        xo = (pick_words(l_offs, "xo_words"), xo_scales)
+        xt = (pick_words(l_two, "xt_words"), xt_scales)
+
+        y_ps = [ps.tile([P, S], F32, name=f"y_ps{t}", tag=f"a{t}") for t in range(4)]
+        for t in range(4):
+            product(y_ps[t][:], w1_q, slice(P * t, P * (t + 1)), xo)
+        for t in range(4):
+            nc.scalar.activation(y_win[t][:, :S], y_ps[t][:], COPY, scale=gain[:, t : t + 1])
+            nc.scalar.activation(st_win[t][:, S:], y_win[t][:].indirect(l_n1[:]), COPY, scale=0.5)
+            nc.vector.scalar_tensor_tensor(st_win[t][:, :S], y_ps[t][:], gain[:, t : t + 1], st_win[t][:, S:], ALU.mult, ALU.add)
+
+        w3_bf = [round_block(w3_raw, u, f"w3_bf{u}") for u in range(4)]
+        w3_q = [quantize(w3_bf[u], f"w3_{u}") for u in range(4)]
+        d_ps = [ps.tile([P, S], F32, name=f"d_ps{u}", tag=f"b{u}") for u in range(4)]
+        for u in range(4):
+            product(d_ps[u][:], w3_q[u], slice(0, P), xt)
+
+        z = sb.tile([P, 4, S], F32, name="z")
+        for t in range(4):
+            g2 = sb.tile([P, S], F32, name=f"g2_{t}")
+            nc.scalar.activation(g2[:], st_win[t][:].indirect(l_n2[:]), COPY)
+            nc.vector.tensor_tensor(z[:, t, :], st_win[t][:, :S], g2[:], ALU.subtract)
+        w2_bf = [round_block(w2_raw, u, f"w2_bf{u}") for u in range(4)]
+        z_bf = sb.tile([P, 4 * S], BF16, name="z_bf", align_bytes=64)
+        nc.vector.tensor_copy(z_bf[:].rearrange("p (c i t) -> p c t i", i=4, t=4), z[:].rearrange("p t (c i) -> p c t i", i=4))
+        w2_q = [quantize(w2_bf[u], f"w2_{u}") for u in range(4)]
+        z_q = quantize(z_bf, "z")
+        h_ps = [ps.tile([P, S], F32, name=f"h_ps{u}", tag=f"a{u}") for u in range(4)]
+        for u in range(4):
+            product(h_ps[u][:], w2_q[u], slice(0, P), z_q)
+
+        for u in range(4):
+            nc.scalar.activation(d_win[u][:, :S], d_ps[u][:], COPY)
+        for u in range(4):
+            nc.vector.tensor_scalar(h_win[u][:, :S], h_ps[u][:], -0.5, None, ALU.mult)
+
+        g4 = [sb.tile([P, S], F32, name=f"g4_{u}") for u in range(4)]
+        g5 = [sb.tile([P, S], F32, name=f"g5_{u}") for u in range(4)]
+        g3 = [sb.tile([P, S], F32, name=f"g3_{u}") for u in range(4)]
+        for u in range(4):
+            if u < 2:
+                nc.scalar.activation(g4[u][:], d_win[u][:].indirect(l_n4[:]), COPY)
+            else:
+                nc.vector.tensor_copy(g4[u][:], d_win[u][:].indirect(l_n4[:]))
+        for u in range(4):
+            nc.scalar.activation(g3[u][:], h_win[u][:].indirect(l_n3[:]), COPY)
+            nc.scalar.activation(g5[u][:], d_win[u][:].indirect(l_n5[:]), COPY)
+            a = sb.tile([P, S], F32, name=f"a_{u}")
+            m = sb.tile([P, S], F32, name=f"m_{u}")
+            o = sb.tile([P, S], F32, name=f"o_{u}")
+            nc.vector.tensor_tensor(a[:], h_ps[u][:], g3[u][:], ALU.add)
+            nc.vector.tensor_tensor(m[:], a[:], g4[u][:], ALU.min)
+            nc.vector.tensor_tensor(o[:], m[:], g5[u][:], ALU.max)
+            nc.sync.dma_start(out[P * u : P * (u + 1), :], o[:])

@@ -16,7 +16,7 @@ P = 128
 K, T, S, N, H = 512, 2048, 256, 512, 512
 FLOPS = 2 * S * (K * H + H * N + K * N)
 W8 = 512
-W1 = 352
+W1 = 512
 
 
 def tile_picked_lateclampbhop_none_p_kernel(tc, x_words, x_scales, w1, gn, w2, w3, offs, n1, n2, two, n3, n4, n5, out):
@@ -35,31 +35,37 @@ def tile_picked_lateclampbhop_none_p_kernel(tc, x_words, x_scales, w1, gn, w2, w
             nc.sync.dma_start(t[:], w.rearrange("(p j) c -> p j c", j=4))
             return t
 
+        def load_halves(w, name):
+            tiles = [sb.tile([P, 1024], F32, name=f"{name}{e}") for e in range(2)]
+            for e in range(2):
+                nc.sync.dma_start(tiles[e][:].rearrange("p (j c) -> p j c", j=4),
+                                  w[:, 256 * e : 256 * (e + 1)].rearrange("(p j) c -> p j c", j=4))
+            return tiles
+
+        xs_in = sb.tile([P, T // 4], I32, name="xs_in")
+        for q in range(4):
+            nc.sync.dma_start(xs_in[32 * q : 32 * q + 4, :], x_scales[0, 4 * q : 4 * q + 4, :].bitcast(I32))
         xs = sb.tile([P, T], U8, name="xs", align_bytes=64)
         nc.vector.memset(xs[:].bitcast(I32), 0)
-        for q in range(4):
-            nc.scalar.dma_start(xs[32 * q : 32 * q + 4, :].bitcast(I32), x_scales[0, 4 * q : 4 * q + 4, :].bitcast(I32))
 
         l_offs = load_list(offs, "l_offs")
-        l_two = load_list(two, "l_two")
         w1_raw = load_weight(w1, "w1_raw")
+        l_two = load_list(two, "l_two")
         xw = sb.tile([P, T], I32, name="xw", align_bytes=64)
         nc.sync.dma_start(xw[:], x_words[0].rearrange("p n t -> p (n t)").bitcast(I32))
         gain = sb.tile([P, 4], F32, name="gain")
         nc.sync.dma_start(gain[:], gn.rearrange("(p t) o -> p (t o)", t=4))
         l_n1 = load_list(n1, "l_n1")
-        w3_raw = load_weight(w3, "w3_raw")
+        w3_raw = load_halves(w3, "w3_raw")
         l_n2 = load_list(n2, "l_n2")
-        w2_raw = load_weight(w2, "w2_raw")
+        w2_raw = load_halves(w2, "w2_raw")
         l_n5 = load_list(n5, "l_n5")
         l_n4 = load_list(n4, "l_n4")
         l_n3 = load_list(n3, "l_n3")
 
         y_win = [sb.tile([P, W8], F32, name=f"y_win{t}") for t in range(4)]
-        st_win = [sb.tile([P, W8], F32, name=f"st_win{t}") for t in range(4)]
-        d_win = [sb.tile([P, W1], F32, name=f"d_win{t}") for t in range(4)]
         h_win = [sb.tile([P, W1], F32, name=f"h_win{t}") for t in range(4)]
-        for win in y_win + d_win + h_win:
+        for win in y_win + h_win:
             nc.vector.memset(win[:, S:], 0.0)
 
         def pick_scales(lst, name):
@@ -76,77 +82,96 @@ def tile_picked_lateclampbhop_none_p_kernel(tc, x_words, x_scales, w1, gn, w2, w
             n = src.shape[1] // 4
             codes = sb.tile([P, n], U32, name=name + "_codes", align_bytes=64)
             scales = sb.tile([P, n], U8, name=name + "_scales", align_bytes=64)
-            nc.vector.quantize_mx(out=codes[:].bitcast(FP8X4), scales=scales[:], in_=src[:])
+            nc.vector.quantize_mx(out=codes[:].bitcast(FP8X4), scales=scales[:], in_=src)
             return codes, scales
 
         def product(acc, lhs, cols, rhs):
             nc.tensor.matmul_mx(out=acc, lhsT=lhs[0][:, cols].bitcast(FP8X4), lhsT_scale=lhs[1][:, cols],
                                 rhs=rhs[0][:].bitcast(FP8X4), rhs_scale=rhs[1][:], start=True, stop=True)
 
-        def round_block(raw, u, name):
-            t = sb.tile([P, 512], BF16, name=name, align_bytes=64)
-            nc.vector.tensor_copy(t[:].rearrange("p (c i j) -> p c j i", i=4, j=4),
-                                  raw[:, :, P * u : P * (u + 1)].rearrange("p j (c i) -> p c j i", i=4))
+        def round_weight(raw, name):
+            t = sb.tile([P, 1024], F32, name=name, align_bytes=64)
+            for e in range(2):
+                nc.vector.tensor_copy(t[:, 512 * e : 512 * (e + 1)].bitcast(BF16).rearrange("p (c i j) -> p c j i", i=4, j=4),
+                                      raw[e][:].rearrange("p (j c i) -> p c j i", i=4, j=4))
             return t
 
+        for q in range(4):
+            nc.vector.tensor_copy(xs[32 * q : 32 * q + 4, :].bitcast(I32), xs_in[32 * q : 32 * q + 4, :])
         xo_scales = pick_scales(l_offs, "xo_scales")
         xt_scales = pick_scales(l_two, "xt_scales")
 
-        w1_bf = sb.tile([P, 2048], BF16, name="w1_bf", align_bytes=64)
-        nc.vector.tensor_copy(w1_bf[:].rearrange("p (t m j) -> p m j t", t=4, j=4),
-                              w1_raw[:].rearrange("p j (m t) -> p m j t", t=4))
-        w1_q = quantize(w1_bf, "w1")
+        w1_bf = [sb.tile([P, 1024], BF16, name=f"w1_bf{e}", align_bytes=64) for e in range(2)]
+        w1_view = w1_raw[:].rearrange("p j (m t) -> p m j t", t=4)
+        nc.scalar.activation(w1_bf[1][:].rearrange("p (t m j) -> p m j t", t=2, j=4), w1_view[:, :, :, 2:4], COPY)
+        nc.vector.tensor_copy(w1_bf[0][:].rearrange("p (t m j) -> p m j t", t=2, j=4), w1_view[:, :, :, 0:2])
+        w1_q = [quantize(w1_bf[e][:], f"w1_{e}") for e in range(2)]
         xo = (pick_words(l_offs, "xo_words"), xo_scales)
         xt = (pick_words(l_two, "xt_words"), xt_scales)
 
         y_ps = [ps.tile([P, S], F32, name=f"y_ps{t}", tag=f"a{t}") for t in range(4)]
         for t in range(4):
-            product(y_ps[t][:], w1_q, slice(P * t, P * (t + 1)), xo)
-        for t in range(4):
-            nc.scalar.activation(y_win[t][:, :S], y_ps[t][:], COPY, scale=gain[:, t : t + 1])
-            nc.scalar.activation(st_win[t][:, S:], y_win[t][:].indirect(l_n1[:]), COPY, scale=0.5)
-            nc.vector.scalar_tensor_tensor(st_win[t][:, :S], y_ps[t][:], gain[:, t : t + 1], st_win[t][:, S:], ALU.mult, ALU.add)
+            product(y_ps[t][:], w1_q[t // 2], slice(P * (t % 2), P * (t % 2 + 1)), xo)
+        g1 = [sb.tile([P, S], F32, name=f"g1_{t}") for t in range(4)]
+        for t in range(5):
+            if t < 2:
+                nc.vector.tensor_scalar(y_win[t][:, :S], y_ps[t][:], gain[:, t : t + 1], None, ALU.mult)
+            elif t < 4:
+                nc.scalar.activation(y_win[t][:, :S], y_ps[t][:], COPY, scale=gain[:, t : t + 1])
+            if t > 0:
+                nc.scalar.activation(g1[t - 1][:], y_win[t - 1][:].indirect(l_n1[:]), COPY, scale=0.5)
 
-        w3_bf = [round_block(w3_raw, u, f"w3_bf{u}") for u in range(4)]
-        w3_q = [quantize(w3_bf[u], f"w3_{u}") for u in range(4)]
+        w3_bf = round_weight(w3_raw, "w3_bf")
+        w3_q = quantize(w3_bf[:].bitcast(BF16), "w3")
         d_ps = [ps.tile([P, S], F32, name=f"d_ps{u}", tag=f"b{u}") for u in range(4)]
         for u in range(4):
-            product(d_ps[u][:], w3_q[u], slice(0, P), xt)
+            product(d_ps[u][:], w3_q, slice(P * u, P * (u + 1)), xt)
+        w2_bf = round_weight(w2_raw, "w2_bf")
+        w2_q = quantize(w2_bf[:].bitcast(BF16), "w2")
 
-        z = sb.tile([P, 4, S], F32, name="z")
+        st_1 = sb.tile([P, W8], F32, name="st_1", tag="w3_bf", align_bytes=64)
+        nc.gpsimd.memset(st_1[:, S:], 0.0)
+        st_win = [w3_raw[1], st_1, w2_raw[0], w2_raw[1]]
+        for t in range(4):
+            nc.vector.scalar_tensor_tensor(st_win[t][:, :S], y_ps[t][:], gain[:, t : t + 1], g1[t][:], ALU.mult, ALU.add)
+        z = w2_bf[:].rearrange("p (t s) -> p t s", t=4)
         for t in range(4):
             g2 = sb.tile([P, S], F32, name=f"g2_{t}")
             nc.scalar.activation(g2[:], st_win[t][:].indirect(l_n2[:]), COPY)
             nc.vector.tensor_tensor(z[:, t, :], st_win[t][:, :S], g2[:], ALU.subtract)
-        w2_bf = [round_block(w2_raw, u, f"w2_bf{u}") for u in range(4)]
+        d_win = st_win
         z_bf = sb.tile([P, 4 * S], BF16, name="z_bf", align_bytes=64)
-        nc.vector.tensor_copy(z_bf[:].rearrange("p (c i t) -> p c t i", i=4, t=4), z[:].rearrange("p t (c i) -> p c t i", i=4))
-        w2_q = [quantize(w2_bf[u], f"w2_{u}") for u in range(4)]
-        z_q = quantize(z_bf, "z")
+        nc.vector.tensor_copy(z_bf[:].rearrange("p (c i t) -> p c t i", i=4, t=4), z.rearrange("p t (c i) -> p c t i", i=4))
+        z_q = quantize(z_bf[:], "z")
         h_ps = [ps.tile([P, S], F32, name=f"h_ps{u}", tag=f"a{u}") for u in range(4)]
         for u in range(4):
-            product(h_ps[u][:], w2_q[u], slice(0, P), z_q)
+            product(h_ps[u][:], w2_q, slice(P * u, P * (u + 1)), z_q)
 
         for u in range(4):
             nc.scalar.activation(d_win[u][:, :S], d_ps[u][:], COPY)
         for u in range(4):
             nc.vector.tensor_scalar(h_win[u][:, :S], h_ps[u][:], -0.5, None, ALU.mult)
 
-        g4 = [sb.tile([P, S], F32, name=f"g4_{u}") for u in range(4)]
-        g5 = [sb.tile([P, S], F32, name=f"g5_{u}") for u in range(4)]
-        g3 = [sb.tile([P, S], F32, name=f"g3_{u}") for u in range(4)]
+        g4_0 = sb.tile([P, S], F32, name="g4_0")
+        g5_0 = sb.tile([P, S], F32, name="g5_0")
+        g4_2 = sb.tile([P, S], F32, name="g4_2", tag="z_bf", align_bytes=64)
+        nc.vector.tensor_copy(g4_2[:], d_win[2][:].indirect(l_n4[:]))
+        g4 = [g4_0[:], h_win[0][:, S:], g4_2[:]]
+        g5 = [g5_0[:]] + [h_win[u][:, S:] for u in range(1, 4)]
         for u in range(4):
+            g3 = sb.tile([P, S], F32, name=f"g3_{u}")
+            nc.scalar.activation(g3[:], h_win[u][:].indirect(l_n3[:]), COPY)
             if u < 2:
-                nc.scalar.activation(g4[u][:], d_win[u][:].indirect(l_n4[:]), COPY)
-            else:
-                nc.vector.tensor_copy(g4[u][:], d_win[u][:].indirect(l_n4[:]))
-        for u in range(4):
-            nc.scalar.activation(g3[u][:], h_win[u][:].indirect(l_n3[:]), COPY)
-            nc.scalar.activation(g5[u][:], d_win[u][:].indirect(l_n5[:]), COPY)
+                nc.scalar.activation(g4[u], d_win[u][:].indirect(l_n4[:]), COPY)
+            nc.scalar.activation(g5[u], d_win[u][:].indirect(l_n5[:]), COPY)
             a = sb.tile([P, S], F32, name=f"a_{u}")
             m = sb.tile([P, S], F32, name=f"m_{u}")
             o = sb.tile([P, S], F32, name=f"o_{u}")
-            nc.vector.tensor_tensor(a[:], h_ps[u][:], g3[u][:], ALU.add)
-            nc.vector.tensor_tensor(m[:], a[:], g4[u][:], ALU.min)
-            nc.vector.tensor_tensor(o[:], m[:], g5[u][:], ALU.max)
+            nc.vector.tensor_tensor(a[:], h_ps[u][:], g3[:], ALU.add)
+            nc.vector.tensor_tensor(m[:], a[:], g4[u], ALU.min)
+            nc.vector.tensor_tensor(o[:], m[:], g5[u], ALU.max)
             nc.sync.dma_start(out[P * u : P * (u + 1), :], o[:])
+            if u == 0:
+                g4_3 = sb.tile([P, S], F32, name="g4_3", tag="a_0")
+                nc.vector.tensor_copy(g4_3[:], d_win[3][:].indirect(l_n4[:]))
+                g4.append(g4_3[:])

@@ -12,166 +12,196 @@ FP8X4 = mybir.dt.float8_e4m3fn_x4
 ALU = mybir.AluOpType
 COPY = mybir.ActivationFunctionType.Copy
 
-P = 128
 K, T, S, N, H = 512, 2048, 256, 512, 512
 FLOPS = 2 * S * (K * H + H * N + K * N)
-W8 = 512
-W1 = 512
+
+P = 128
+PACK = 4
+LINE = 4
+HALF = 256
 
 
-def tile_picked_lateclampbhop_none_p_kernel(tc, x_words, x_scales, w1, gn, w2, w3, offs, n1, n2, two, n3, n4, n5, out):
+def tile_picked_lateclampbhop_none_p_kernel(
+    tc, x_words, x_scales, w1, gn, w2, w3, offs, n1, n2, two, n3, n4, n5, out
+):
     nc = tc.nc
     with ExitStack() as ctx:
         sb = ctx.enter_context(tc.tile_pool(name="sb", bufs=1))
         ps = ctx.enter_context(tc.psum_pool(name="ps", bufs=1))
 
-        def load_list(ap, name):
-            t = sb.tile([P, S // 16], U16, name=name)
-            nc.sync.dma_start(t[:], ap)
-            return t
-
-        def load_weight(w, name):
-            t = sb.tile([P, 4, 512], F32, name=name)
-            nc.sync.dma_start(t[:], w.rearrange("(p j) c -> p j c", j=4))
-            return t
+        def load_list(entries, name):
+            tile = sb.tile([P, S // 16], U16, name=name)
+            nc.sync.dma_start(tile[:], entries)
+            return tile
 
         def load_halves(w, name):
-            tiles = [sb.tile([P, 1024], F32, name=f"{name}{e}") for e in range(2)]
+            tiles = [sb.tile([P, PACK * HALF], F32, name=f"{name}{e}") for e in range(2)]
             for e in range(2):
-                nc.sync.dma_start(tiles[e][:].rearrange("p (j c) -> p j c", j=4),
-                                  w[:, 256 * e : 256 * (e + 1)].rearrange("(p j) c -> p j c", j=4))
+                nc.sync.dma_start(
+                    tiles[e][:].rearrange("p (j c) -> p j c", j=PACK),
+                    w[:, HALF * e : HALF * (e + 1)].rearrange("(p j) c -> p j c", j=PACK),
+                )
             return tiles
 
-        xs_in = sb.tile([P, T // 4], I32, name="xs_in")
-        for q in range(4):
-            nc.sync.dma_start(xs_in[32 * q : 32 * q + 4, :], x_scales[0, 4 * q : 4 * q + 4, :].bitcast(I32))
-        xs = sb.tile([P, T], U8, name="xs", align_bytes=64)
-        nc.vector.memset(xs[:].bitcast(I32), 0)
+        scale_rows = sb.tile([P, T // 4], I32, name="scale_rows")
+        for q in range(PACK):
+            queue = nc.scalar if q < PACK // 2 else nc.sync
+            queue.dma_start(scale_rows[32 * q : 32 * q + 4, :], x_scales[0, 4 * q : 4 * q + 4, :].bitcast(I32))
+        scale_table = sb.tile([P, T], U8, name="scale_table", align_bytes=64)
+        nc.gpsimd.memset(scale_table[:].bitcast(I32), 0)
 
-        l_offs = load_list(offs, "l_offs")
-        w1_raw = load_weight(w1, "w1_raw")
-        l_two = load_list(two, "l_two")
-        xw = sb.tile([P, T], I32, name="xw", align_bytes=64)
-        nc.sync.dma_start(xw[:], x_words[0].rearrange("p n t -> p (n t)").bitcast(I32))
-        gain = sb.tile([P, 4], F32, name="gain")
-        nc.sync.dma_start(gain[:], gn.rearrange("(p t) o -> p (t o)", t=4))
-        l_n1 = load_list(n1, "l_n1")
+        offs_sb = load_list(offs, "offs_sb")
+        w1_raw = sb.tile([P, PACK, H], F32, name="w1_raw")
+        nc.sync.dma_start(w1_raw[:], w1.rearrange("(p j) c -> p j c", j=PACK))
+        two_sb = load_list(two, "two_sb")
+        word_table = sb.tile([P, T], I32, name="word_table", align_bytes=64)
+        nc.sync.dma_start(word_table[:], x_words[0].rearrange("p n t -> p (n t)").bitcast(I32))
+        gain = sb.tile([P, PACK], F32, name="gain")
+        nc.sync.dma_start(gain[:], gn.rearrange("(p t) o -> p (t o)", t=PACK))
+        n1_sb = load_list(n1, "n1_sb")
         w3_raw = load_halves(w3, "w3_raw")
-        l_n2 = load_list(n2, "l_n2")
+        n2_sb = load_list(n2, "n2_sb")
         w2_raw = load_halves(w2, "w2_raw")
-        l_n5 = load_list(n5, "l_n5")
-        l_n4 = load_list(n4, "l_n4")
-        l_n3 = load_list(n3, "l_n3")
+        n5_sb = load_list(n5, "n5_sb")
+        n4_sb = load_list(n4, "n4_sb")
+        n3_sb = load_list(n3, "n3_sb")
 
-        y_win = [sb.tile([P, W8], F32, name=f"y_win{t}") for t in range(4)]
-        h_win = [sb.tile([P, W1], F32, name=f"h_win{t}") for t in range(4)]
-        for win in y_win + h_win:
-            nc.vector.memset(win[:, S:], 0.0)
+        y_win = [sb.tile([P, 2 * S], F32, name=f"y_win{t}") for t in range(PACK)]
+        late = sb.tile([P, 10 * S], F32, name="late", align_bytes=64)
+        for win in y_win:
+            nc.gpsimd.memset(win[:, S:], 0.0)
+        nc.gpsimd.memset(late[:, 4 * S : 5 * S], 0.0)
+        nc.gpsimd.memset(late[:, 7 * S :], 0.0)
 
-        def pick_scales(lst, name):
-            t = sb.tile([P, S], U8, name=name, align_bytes=64)
-            nc.vector.tensor_copy(t[:], xs[:].indirect(lst[:]))
-            return t
+        def slot(first, count=1):
+            return late[:, first * S : (first + count) * S]
 
-        def pick_words(lst, name):
-            t = sb.tile([P, S], U32, name=name, align_bytes=64)
-            nc.vector.tensor_copy(t[:], xw[:].bitcast(U32).indirect(lst[:]))
-            return t
+        def pick_scales(entries, name):
+            tile = sb.tile([P, S], U8, name=name, align_bytes=64)
+            nc.vector.tensor_copy(tile[:], scale_table[:].indirect(entries[:]))
+            return tile
+
+        def pick_words(entries, name):
+            tile = sb.tile([P, S], U32, name=name, align_bytes=64)
+            nc.vector.tensor_copy(tile[:], word_table[:].bitcast(U32).indirect(entries[:]))
+            return tile
 
         def quantize(src, name):
-            n = src.shape[1] // 4
-            codes = sb.tile([P, n], U32, name=name + "_codes", align_bytes=64)
-            scales = sb.tile([P, n], U8, name=name + "_scales", align_bytes=64)
-            nc.vector.quantize_mx(out=codes[:].bitcast(FP8X4), scales=scales[:], in_=src)
-            return codes, scales
+            width = src.shape[1] // PACK
+            words = sb.tile([P, width], U32, name=name + "_words", align_bytes=64)
+            scales = sb.tile([P, width], U8, name=name + "_scales", align_bytes=64)
+            nc.vector.quantize_mx(out=words[:].bitcast(FP8X4), scales=scales[:], in_=src)
+            return words, scales
 
-        def product(acc, lhs, cols, rhs):
-            nc.tensor.matmul_mx(out=acc, lhsT=lhs[0][:, cols].bitcast(FP8X4), lhsT_scale=lhs[1][:, cols],
-                                rhs=rhs[0][:].bitcast(FP8X4), rhs_scale=rhs[1][:], start=True, stop=True)
+        def product(acc, weights, first, moving):
+            cols = slice(first, first + P)
+            nc.tensor.matmul_mx(
+                out=acc,
+                lhsT=weights[0][:, cols].bitcast(FP8X4),
+                lhsT_scale=weights[1][:, cols],
+                rhs=moving[0][:].bitcast(FP8X4),
+                rhs_scale=moving[1][:],
+                start=True,
+                stop=True,
+            )
 
         def round_weight(raw, name):
-            t = sb.tile([P, 1024], F32, name=name, align_bytes=64)
+            tile = sb.tile([P, PACK * N // 2], F32, name=name, align_bytes=64)
             for e in range(2):
-                nc.vector.tensor_copy(t[:, 512 * e : 512 * (e + 1)].bitcast(BF16).rearrange("p (c i j) -> p c j i", i=4, j=4),
-                                      raw[e][:].rearrange("p (j c i) -> p c j i", i=4, j=4))
-            return t
+                half = tile[:, 2 * HALF * e : 2 * HALF * (e + 1)].bitcast(BF16)
+                nc.vector.tensor_copy(
+                    half.rearrange("p (c i j) -> p c j i", i=LINE, j=PACK),
+                    raw[e][:].rearrange("p (j c i) -> p c j i", i=LINE, j=PACK),
+                )
+            return tile
 
-        for q in range(4):
-            nc.vector.tensor_copy(xs[32 * q : 32 * q + 4, :].bitcast(I32), xs_in[32 * q : 32 * q + 4, :])
-        xo_scales = pick_scales(l_offs, "xo_scales")
-        xt_scales = pick_scales(l_two, "xt_scales")
+        for q in range(PACK):
+            nc.vector.tensor_copy(scale_table[32 * q : 32 * q + 4, :].bitcast(I32), scale_rows[32 * q : 32 * q + 4, :])
+        offs_scales = pick_scales(offs_sb, "offs_scales")
+        two_scales = pick_scales(two_sb, "two_scales")
 
-        w1_bf = [sb.tile([P, 1024], BF16, name=f"w1_bf{e}", align_bytes=64) for e in range(2)]
-        w1_view = w1_raw[:].rearrange("p j (m t) -> p m j t", t=4)
-        nc.scalar.activation(w1_bf[1][:].rearrange("p (t m j) -> p m j t", t=2, j=4), w1_view[:, :, :, 2:4], COPY)
-        nc.vector.tensor_copy(w1_bf[0][:].rearrange("p (t m j) -> p m j t", t=2, j=4), w1_view[:, :, :, 0:2])
+        w1_bf = [sb.tile([P, 2 * P * PACK], BF16, name=f"w1_bf{e}", align_bytes=64) for e in range(2)]
+        w1_dealt = [tile[:].rearrange("p (t m j) -> p m j t", t=2, j=PACK) for tile in w1_bf]
+        w1_view = w1_raw[:].rearrange("p j (m t) -> p m j t", t=PACK)
+        nc.scalar.activation(w1_dealt[1], w1_view[:, :, :, 2:4], COPY)
+        nc.vector.tensor_copy(w1_dealt[0], w1_view[:, :, :, 0:2])
         w1_q = [quantize(w1_bf[e][:], f"w1_{e}") for e in range(2)]
-        xo = (pick_words(l_offs, "xo_words"), xo_scales)
-        xt = (pick_words(l_two, "xt_words"), xt_scales)
+        x_offs = (pick_words(offs_sb, "offs_words"), offs_scales)
+        x_two = (pick_words(two_sb, "two_words"), two_scales)
 
-        y_ps = [ps.tile([P, S], F32, name=f"y_ps{t}", tag=f"a{t}") for t in range(4)]
-        for t in range(4):
-            product(y_ps[t][:], w1_q[t // 2], slice(P * (t % 2), P * (t % 2 + 1)), xo)
-        g1 = [sb.tile([P, S], F32, name=f"g1_{t}") for t in range(4)]
-        for t in range(5):
-            if t < 2:
-                nc.vector.tensor_scalar(y_win[t][:, :S], y_ps[t][:], gain[:, t : t + 1], None, ALU.mult)
-            elif t < 4:
+        y_ps = [ps.tile([P, S], F32, name=f"y_ps{t}", tag=f"bank{t}") for t in range(PACK)]
+        for t in range(PACK):
+            product(y_ps[t][:], w1_q[t // 2], P * (t % 2), x_offs)
+
+        y_n1 = [sb.tile([P, S], F32, name=f"y_n1_{t}") for t in range(PACK)]
+        for t in range(PACK + 1):
+            if t < PACK:
                 nc.scalar.activation(y_win[t][:, :S], y_ps[t][:], COPY, scale=gain[:, t : t + 1])
             if t > 0:
-                nc.scalar.activation(g1[t - 1][:], y_win[t - 1][:].indirect(l_n1[:]), COPY, scale=0.5)
+                nc.scalar.activation(y_n1[t - 1][:], y_win[t - 1][:].indirect(n1_sb[:]), COPY, scale=0.5)
 
         w3_bf = round_weight(w3_raw, "w3_bf")
         w3_q = quantize(w3_bf[:].bitcast(BF16), "w3")
-        d_ps = [ps.tile([P, S], F32, name=f"d_ps{u}", tag=f"b{u}") for u in range(4)]
-        for u in range(4):
-            product(d_ps[u][:], w3_q, slice(P * u, P * (u + 1)), xt)
+        d_ps = [ps.tile([P, 2 * S], F32, name=f"d_ps{e}") for e in range(2)]
+        for u in range(PACK):
+            product(d_ps[u // 2][:, (u % 2) * S : (u % 2 + 1) * S], w3_q, P * u, x_two)
         w2_bf = round_weight(w2_raw, "w2_bf")
         w2_q = quantize(w2_bf[:].bitcast(BF16), "w2")
 
-        st_1 = sb.tile([P, W8], F32, name="st_1", tag="w3_bf", align_bytes=64)
+        st_1 = sb.tile([P, 2 * S], F32, name="st_1", tag="w3_bf", align_bytes=64)
         nc.gpsimd.memset(st_1[:, S:], 0.0)
         st_win = [w3_raw[1], st_1, w2_raw[0], w2_raw[1]]
-        for t in range(4):
-            nc.vector.scalar_tensor_tensor(st_win[t][:, :S], y_ps[t][:], gain[:, t : t + 1], g1[t][:], ALU.mult, ALU.add)
-        z = w2_bf[:].rearrange("p (t s) -> p t s", t=4)
-        for t in range(4):
-            g2 = sb.tile([P, S], F32, name=f"g2_{t}")
-            nc.scalar.activation(g2[:], st_win[t][:].indirect(l_n2[:]), COPY)
-            nc.vector.tensor_tensor(z[:, t, :], st_win[t][:, :S], g2[:], ALU.subtract)
-        d_win = st_win
-        z_bf = sb.tile([P, 4 * S], BF16, name="z_bf", align_bytes=64)
-        nc.vector.tensor_copy(z_bf[:].rearrange("p (c i t) -> p c t i", i=4, t=4), z.rearrange("p t (c i) -> p c t i", i=4))
-        z_q = quantize(z_bf[:], "z")
-        h_ps = [ps.tile([P, S], F32, name=f"h_ps{u}", tag=f"a{u}") for u in range(4)]
-        for u in range(4):
-            product(h_ps[u][:], w2_q, slice(P * u, P * (u + 1)), z_q)
+        for t in range(PACK):
+            nc.vector.scalar_tensor_tensor(st_win[t][:, :S], y_ps[t][:], gain[:, t : t + 1], y_n1[t][:], ALU.mult, ALU.add)
+        z = w2_bf[:].rearrange("p (t s) -> p t s", t=PACK)
+        for t in range(PACK):
+            st_n2 = sb.tile([P, S], F32, name=f"st_n2_{t}")
+            nc.scalar.activation(st_n2[:], st_win[t][:].indirect(n2_sb[:]), COPY)
+            nc.vector.tensor_tensor(z[:, t, :], st_win[t][:, :S], st_n2[:], ALU.subtract)
 
-        for u in range(4):
-            nc.scalar.activation(d_win[u][:, :S], d_ps[u][:], COPY)
-        for u in range(4):
-            nc.vector.tensor_scalar(h_win[u][:, :S], h_ps[u][:], -0.5, None, ALU.mult)
+        z_bf = slot(0, 2).bitcast(BF16)
+        nc.vector.tensor_copy(
+            z_bf.rearrange("p (c i t) -> p c t i", i=LINE, t=PACK), z.rearrange("p t (c i) -> p c t i", i=LINE)
+        )
+        z_q = quantize(z_bf, "z")
 
-        g4_0 = sb.tile([P, S], F32, name="g4_0")
-        g5_0 = sb.tile([P, S], F32, name="g5_0")
-        g4_2 = sb.tile([P, S], F32, name="g4_2", tag="z_bf", align_bytes=64)
-        nc.vector.tensor_copy(g4_2[:], d_win[2][:].indirect(l_n4[:]))
-        g4 = [g4_0[:], h_win[0][:, S:], g4_2[:]]
-        g5 = [g5_0[:]] + [h_win[u][:, S:] for u in range(1, 4)]
-        for u in range(4):
-            g3 = sb.tile([P, S], F32, name=f"g3_{u}")
-            nc.scalar.activation(g3[:], h_win[u][:].indirect(l_n3[:]), COPY)
+        h_lo = [ps.tile([P, S], F32, name=f"h_ps{u}", tag=f"bank{u}") for u in range(2)]
+        h_hi = ps.tile([P, 2 * S], F32, name="h_hi")
+        h_ps = [h_lo[0][:], h_lo[1][:], h_hi[:, :S], h_hi[:, S:]]
+        for u in range(PACK):
+            product(h_ps[u], w2_q, P * u, z_q)
+
+        nc.scalar.activation(st_win[3][:, S : 3 * S], d_ps[0][:], COPY)
+        nc.vector.tensor_copy(slot(0, 2), d_ps[1][:])
+        d_win = [st_win[3][:, S : 3 * S], st_win[3][:, 2 * S : 4 * S], slot(0, 3), slot(1, 2)]
+        h_win = [slot(3, 2), slot(2, 2), slot(5, 2), slot(6, 4)]
+        picked = sb.tile([P, 5, S], F32, name="picked")
+        d_n4 = [picked[:, 0, :], picked[:, 2, :], picked[:, 4, :], slot(8)]
+        d_n5 = [picked[:, 1, :], picked[:, 3, :], slot(7), slot(9)]
+        nc.vector.tensor_scalar(slot(3), h_ps[0], -0.5, None, ALU.mult)
+        nc.vector.tensor_scalar(slot(2), h_ps[1], -0.5, None, ALU.mult)
+        nc.vector.tensor_scalar(slot(5, 2), h_hi[:], -0.5, None, ALU.mult)
+        nc.vector.tensor_copy(d_n4[2], d_win[2].indirect(n4_sb[:]))
+
+        h_n3 = sb.tile([P, PACK * S], F32, name="h_n3")
+        for u in range(PACK):
+            nc.scalar.activation(h_n3[:, u * S : (u + 1) * S], h_win[u].indirect(n3_sb[:]), COPY)
+        for u in range(2):
+            nc.scalar.activation(d_n4[u], d_win[u].indirect(n4_sb[:]), COPY)
+            nc.scalar.activation(d_n5[u], d_win[u].indirect(n5_sb[:]), COPY)
+        nc.scalar.activation(d_n5[2], d_win[2].indirect(n5_sb[:]), COPY)
+        nc.scalar.activation(d_n4[3], d_win[3].indirect(n4_sb[:]), COPY)
+        nc.scalar.activation(d_n5[3], d_win[3].indirect(n5_sb[:]), COPY)
+
+        diff = sb.tile([P, PACK * S], F32, name="diff")
+        capped = sb.tile([P, PACK * S], F32, name="capped")
+        result = sb.tile([P, PACK * S], F32, name="result")
+        for u in range(PACK):
+            cols = slice(u * S, (u + 1) * S)
             if u < 2:
-                nc.scalar.activation(g4[u], d_win[u][:].indirect(l_n4[:]), COPY)
-            nc.scalar.activation(g5[u], d_win[u][:].indirect(l_n5[:]), COPY)
-            a = sb.tile([P, S], F32, name=f"a_{u}")
-            m = sb.tile([P, S], F32, name=f"m_{u}")
-            o = sb.tile([P, S], F32, name=f"o_{u}")
-            nc.vector.tensor_tensor(a[:], h_ps[u][:], g3[:], ALU.add)
-            nc.vector.tensor_tensor(m[:], a[:], g4[u], ALU.min)
-            nc.vector.tensor_tensor(o[:], m[:], g5[u], ALU.max)
-            nc.sync.dma_start(out[P * u : P * (u + 1), :], o[:])
-            if u == 0:
-                g4_3 = sb.tile([P, S], F32, name="g4_3", tag="a_0")
-                nc.vector.tensor_copy(g4_3[:], d_win[3][:].indirect(l_n4[:]))
-                g4.append(g4_3[:])
+                nc.vector.tensor_tensor(diff[:, cols], h_ps[u], h_n3[:, cols], ALU.add)
+            elif u == 2:
+                nc.vector.tensor_tensor(diff[:, 2 * S :], h_hi[:], h_n3[:, 2 * S :], ALU.add)
+            nc.vector.tensor_tensor(capped[:, cols], diff[:, cols], d_n4[u], ALU.min)
+            nc.vector.tensor_tensor(result[:, cols], capped[:, cols], d_n5[u], ALU.max)
+            nc.sync.dma_start(out[P * u : P * (u + 1), :], result[:, cols])

from contextlib import ExitStack

import concourse.mybir as mybir

F32 = mybir.dt.float32
BF16 = mybir.dt.bfloat16
I32 = mybir.dt.int32
U32 = mybir.dt.uint32
U16 = mybir.dt.uint16
U8 = mybir.dt.uint8
FP8X4 = mybir.dt.float8_e4m3fn_x4
ALU = mybir.AluOpType
COPY = mybir.ActivationFunctionType.Copy

K, T, S, N, H = 512, 2048, 256, 512, 512
FLOPS = 2 * S * (K * H + H * N + K * N)

P = 128
PACK = 4
LINE = 4
HALF = 256


def tile_picked_lateclampbhop_none_p_kernel(
    tc, x_words, x_scales, w1, gn, w2, w3, offs, n1, n2, two, n3, n4, n5, out
):
    nc = tc.nc
    with ExitStack() as ctx:
        sb = ctx.enter_context(tc.tile_pool(name="sb", bufs=1))
        ps = ctx.enter_context(tc.psum_pool(name="ps", bufs=1))

        def load_list(entries, name):
            tile = sb.tile([P, S // 16], U16, name=name)
            nc.sync.dma_start(tile[:], entries)
            return tile

        def load_halves(w, name):
            tiles = [sb.tile([P, PACK * HALF], F32, name=f"{name}{e}") for e in range(2)]
            for e in range(2):
                nc.sync.dma_start(
                    tiles[e][:].rearrange("p (j c) -> p j c", j=PACK),
                    w[:, HALF * e : HALF * (e + 1)].rearrange("(p j) c -> p j c", j=PACK),
                )
            return tiles

        scale_rows = sb.tile([P, T // 4], I32, name="scale_rows")
        for q in range(PACK):
            queue = nc.scalar if q < PACK // 2 else nc.sync
            queue.dma_start(scale_rows[32 * q : 32 * q + 4, :], x_scales[0, 4 * q : 4 * q + 4, :].bitcast(I32))
        scale_table = sb.tile([P, T], U8, name="scale_table", align_bytes=64)
        nc.gpsimd.memset(scale_table[:].bitcast(I32), 0)

        offs_sb = load_list(offs, "offs_sb")
        w1_raw = sb.tile([P, PACK, H], F32, name="w1_raw")
        nc.sync.dma_start(w1_raw[:], w1.rearrange("(p j) c -> p j c", j=PACK))
        two_sb = load_list(two, "two_sb")
        word_table = sb.tile([P, T], I32, name="word_table", align_bytes=64)
        nc.sync.dma_start(word_table[:], x_words[0].rearrange("p n t -> p (n t)").bitcast(I32))
        gain = sb.tile([P, PACK], F32, name="gain")
        nc.sync.dma_start(gain[:], gn.rearrange("(p t) o -> p (t o)", t=PACK))
        n1_sb = load_list(n1, "n1_sb")
        w3_raw = load_halves(w3, "w3_raw")
        n2_sb = load_list(n2, "n2_sb")
        w2_raw = load_halves(w2, "w2_raw")
        n5_sb = load_list(n5, "n5_sb")
        n4_sb = load_list(n4, "n4_sb")
        n3_sb = load_list(n3, "n3_sb")

        y_win = [sb.tile([P, 2 * S], F32, name=f"y_win{t}") for t in range(PACK)]
        late = sb.tile([P, 10 * S], F32, name="late", align_bytes=64)
        for win in y_win:
            nc.gpsimd.memset(win[:, S:], 0.0)
        nc.gpsimd.memset(late[:, 4 * S : 5 * S], 0.0)
        nc.gpsimd.memset(late[:, 7 * S :], 0.0)

        def slot(first, count=1):
            return late[:, first * S : (first + count) * S]

        def pick_scales(entries, name):
            tile = sb.tile([P, S], U8, name=name, align_bytes=64)
            nc.vector.tensor_copy(tile[:], scale_table[:].indirect(entries[:]))
            return tile

        def pick_words(entries, name):
            tile = sb.tile([P, S], U32, name=name, align_bytes=64)
            nc.vector.tensor_copy(tile[:], word_table[:].bitcast(U32).indirect(entries[:]))
            return tile

        def quantize(src, name):
            width = src.shape[1] // PACK
            words = sb.tile([P, width], U32, name=name + "_words", align_bytes=64)
            scales = sb.tile([P, width], U8, name=name + "_scales", align_bytes=64)
            nc.vector.quantize_mx(out=words[:].bitcast(FP8X4), scales=scales[:], in_=src)
            return words, scales

        def product(acc, weights, first, moving):
            cols = slice(first, first + P)
            nc.tensor.matmul_mx(
                out=acc,
                lhsT=weights[0][:, cols].bitcast(FP8X4),
                lhsT_scale=weights[1][:, cols],
                rhs=moving[0][:].bitcast(FP8X4),
                rhs_scale=moving[1][:],
                start=True,
                stop=True,
            )

        def round_weight(raw, name):
            tile = sb.tile([P, PACK * N // 2], F32, name=name, align_bytes=64)
            for e in range(2):
                half = tile[:, 2 * HALF * e : 2 * HALF * (e + 1)].bitcast(BF16)
                nc.vector.tensor_copy(
                    half.rearrange("p (c i j) -> p c j i", i=LINE, j=PACK),
                    raw[e][:].rearrange("p (j c i) -> p c j i", i=LINE, j=PACK),
                )
            return tile

        for q in range(PACK):
            nc.vector.tensor_copy(scale_table[32 * q : 32 * q + 4, :].bitcast(I32), scale_rows[32 * q : 32 * q + 4, :])
        offs_scales = pick_scales(offs_sb, "offs_scales")
        two_scales = pick_scales(two_sb, "two_scales")

        w1_bf = [sb.tile([P, 2 * P * PACK], BF16, name=f"w1_bf{e}", align_bytes=64) for e in range(2)]
        w1_dealt = [tile[:].rearrange("p (t m j) -> p m j t", t=2, j=PACK) for tile in w1_bf]
        w1_view = w1_raw[:].rearrange("p j (m t) -> p m j t", t=PACK)
        nc.scalar.activation(w1_dealt[1], w1_view[:, :, :, 2:4], COPY)
        nc.vector.tensor_copy(w1_dealt[0], w1_view[:, :, :, 0:2])
        w1_q = [quantize(w1_bf[e][:], f"w1_{e}") for e in range(2)]
        x_offs = (pick_words(offs_sb, "offs_words"), offs_scales)
        x_two = (pick_words(two_sb, "two_words"), two_scales)

        y_ps = [ps.tile([P, S], F32, name=f"y_ps{t}", tag=f"bank{t}") for t in range(PACK)]
        for t in range(PACK):
            product(y_ps[t][:], w1_q[t // 2], P * (t % 2), x_offs)

        y_n1 = [sb.tile([P, S], F32, name=f"y_n1_{t}") for t in range(PACK)]
        for t in range(PACK + 1):
            if t < PACK:
                nc.scalar.activation(y_win[t][:, :S], y_ps[t][:], COPY, scale=gain[:, t : t + 1])
            if t > 0:
                nc.scalar.activation(y_n1[t - 1][:], y_win[t - 1][:].indirect(n1_sb[:]), COPY, scale=0.5)

        w3_bf = round_weight(w3_raw, "w3_bf")
        w3_q = quantize(w3_bf[:].bitcast(BF16), "w3")
        d_ps = [ps.tile([P, 2 * S], F32, name=f"d_ps{e}") for e in range(2)]
        for u in range(PACK):
            product(d_ps[u // 2][:, (u % 2) * S : (u % 2 + 1) * S], w3_q, P * u, x_two)
        w2_bf = round_weight(w2_raw, "w2_bf")
        w2_q = quantize(w2_bf[:].bitcast(BF16), "w2")

        st_1 = sb.tile([P, 2 * S], F32, name="st_1", tag="w3_bf", align_bytes=64)
        nc.gpsimd.memset(st_1[:, S:], 0.0)
        st_win = [w3_raw[1], st_1, w2_raw[0], w2_raw[1]]
        for t in range(PACK):
            nc.vector.scalar_tensor_tensor(st_win[t][:, :S], y_ps[t][:], gain[:, t : t + 1], y_n1[t][:], ALU.mult, ALU.add)
        z = w2_bf[:].rearrange("p (t s) -> p t s", t=PACK)
        for t in range(PACK):
            st_n2 = sb.tile([P, S], F32, name=f"st_n2_{t}")
            nc.scalar.activation(st_n2[:], st_win[t][:].indirect(n2_sb[:]), COPY)
            nc.vector.tensor_tensor(z[:, t, :], st_win[t][:, :S], st_n2[:], ALU.subtract)

        z_bf = slot(0, 2).bitcast(BF16)
        nc.vector.tensor_copy(
            z_bf.rearrange("p (c i t) -> p c t i", i=LINE, t=PACK), z.rearrange("p t (c i) -> p c t i", i=LINE)
        )
        z_q = quantize(z_bf, "z")

        h_lo = [ps.tile([P, S], F32, name=f"h_ps{u}", tag=f"bank{u}") for u in range(2)]
        h_hi = ps.tile([P, 2 * S], F32, name="h_hi")
        h_ps = [h_lo[0][:], h_lo[1][:], h_hi[:, :S], h_hi[:, S:]]
        for u in range(PACK):
            product(h_ps[u], w2_q, P * u, z_q)

        nc.scalar.activation(st_win[3][:, S : 3 * S], d_ps[0][:], COPY)
        nc.vector.tensor_copy(slot(0, 2), d_ps[1][:])
        d_win = [st_win[3][:, S : 3 * S], st_win[3][:, 2 * S : 4 * S], slot(0, 3), slot(1, 2)]
        h_win = [slot(3, 2), slot(2, 2), slot(5, 2), slot(6, 4)]
        picked = sb.tile([P, 5, S], F32, name="picked")
        d_n4 = [picked[:, 0, :], picked[:, 2, :], picked[:, 4, :], slot(8)]
        d_n5 = [picked[:, 1, :], picked[:, 3, :], slot(7), slot(9)]
        nc.vector.tensor_scalar(slot(3), h_ps[0], -0.5, None, ALU.mult)
        nc.vector.tensor_scalar(slot(2), h_ps[1], -0.5, None, ALU.mult)
        nc.vector.tensor_scalar(slot(5, 2), h_hi[:], -0.5, None, ALU.mult)
        nc.vector.tensor_copy(d_n4[2], d_win[2].indirect(n4_sb[:]))

        h_n3 = sb.tile([P, PACK * S], F32, name="h_n3")
        for u in range(PACK):
            nc.scalar.activation(h_n3[:, u * S : (u + 1) * S], h_win[u].indirect(n3_sb[:]), COPY)
        for u in range(2):
            nc.scalar.activation(d_n4[u], d_win[u].indirect(n4_sb[:]), COPY)
            nc.scalar.activation(d_n5[u], d_win[u].indirect(n5_sb[:]), COPY)
        nc.scalar.activation(d_n5[2], d_win[2].indirect(n5_sb[:]), COPY)
        nc.scalar.activation(d_n4[3], d_win[3].indirect(n4_sb[:]), COPY)
        nc.scalar.activation(d_n5[3], d_win[3].indirect(n5_sb[:]), COPY)

        diff = sb.tile([P, PACK * S], F32, name="diff")
        capped = sb.tile([P, PACK * S], F32, name="capped")
        result = sb.tile([P, PACK * S], F32, name="result")
        for u in range(PACK):
            cols = slice(u * S, (u + 1) * S)
            if u < 2:
                nc.vector.tensor_tensor(diff[:, cols], h_ps[u], h_n3[:, cols], ALU.add)
            elif u == 2:
                nc.vector.tensor_tensor(diff[:, 2 * S :], h_hi[:], h_n3[:, 2 * S :], ALU.add)
            nc.vector.tensor_tensor(capped[:, cols], diff[:, cols], d_n4[u], ALU.min)
            nc.vector.tensor_tensor(result[:, cols], capped[:, cols], d_n5[u], ALU.max)
            nc.sync.dma_start(out[P * u : P * (u + 1), :], result[:, cols])
